import numpy as np
import ml_dtypes


def mxq(x, axis, fmt="e4m3"):
    dtype, down = {"e4m3": (ml_dtypes.float8_e4m3fn, 7), "e5m2": (ml_dtypes.float8_e5m2, 14)}[fmt]
    v = np.moveaxis(np.asarray(x, np.float32).astype(ml_dtypes.bfloat16).astype(np.float64), axis, -1)
    blocks = v.reshape(v.shape[:-1] + (-1, 32))
    amax = np.abs(blocks).max(-1, keepdims=True)
    byte = np.maximum(np.where(amax > 0, np.frexp(amax)[1] - 1 + 127, 0) - down, 1)
    scale = np.exp2(byte - 127.0)
    codes = (blocks / scale).astype(np.float32).astype(dtype).astype(np.float64)
    return np.moveaxis((codes * scale).reshape(v.shape), -1, axis)


WIDE = False


def mx_kscale(k):
    if not WIDE:
        return np.ones(k)
    levels = np.array([10, -10, 5, -5, 0])
    if k % 512:
        return np.exp2(np.random.permutation(np.resize(levels, k // 32))).repeat(32)
    a = np.empty((k // 512, 16))
    for p in range(k // 512):
        a[p, :8] = np.random.permutation(np.resize(levels, 8))
        for g in range(8):
            far = levels[np.abs(levels - a[p, g]) >= 10]
            a[p, g + 8] = far[np.random.randint(len(far))]
    return np.exp2(a.ravel()).repeat(32)


def f64(x):
    return np.asarray(x).astype(np.float64)


def striped(idx):
    return np.tile(idx.reshape(-1, 16).T, (8, 1)).astype(np.uint16)


def unstriped(offs):
    return offs[:16].T.reshape(-1).astype(np.int64)


E2M1 = np.array([0.0, 0.5, 1.0, 1.5, 2.0, 3.0, 4.0, 6.0, -0.0, -0.5, -1.0, -1.5, -2.0, -3.0, -4.0, -6.0])


def pack_weight(w, fmt):
    k, n = w.shape
    w = f64(np.asarray(w, np.float32).astype(ml_dtypes.bfloat16)).reshape(k // 32, 32, n)
    amax = np.abs(w).max(1)
    if fmt == "e4m3":
        byte = np.frexp(amax)[1] - 1 + 127 - 7
    else:
        mant, ex = np.frexp(amax / 6.0)
        byte = np.where(mant > 0.5, ex, ex - 1) + 127
    byte = np.clip(np.where(amax > 0, byte, 1), 1, 254)
    scaled = (w * np.exp2(127.0 - byte)[:, None, :]).reshape(k, n).astype(np.float32)
    by_word = np.ascontiguousarray(scaled.reshape(k // 512, 128, 4, n).transpose(0, 1, 3, 2))
    if fmt == "e4m3":
        words = by_word.astype(ml_dtypes.float8_e4m3fn).view(np.uint8)
    else:
        c = by_word.astype(ml_dtypes.float4_e2m1fn).view(np.uint8) & 0xF
        words = (c[..., 0::2] | (c[..., 1::2] << 4)).reshape(k // 512, 128, 2 * n)
    return np.ascontiguousarray(words), np.ascontiguousarray(byte.astype(np.uint8).reshape(k // 512, 16, n))


def unpack_weight(words, scales, fmt):
    g, _, n = scales.shape
    words = np.ascontiguousarray(words).reshape(g, 128, n, -1)
    if fmt == "e4m3":
        vals = words.view(ml_dtypes.float8_e4m3fn).astype(np.float64)
    else:
        nib = np.empty((g, 128, n, 4), np.uint8)
        nib[..., 0::2] = words & 0xF
        nib[..., 1::2] = words >> 4
        vals = E2M1[nib]
    vals = vals * np.repeat(np.exp2(scales.astype(np.float64) - 127.0), 8, axis=1)[..., None]
    return vals.transpose(0, 1, 3, 2).reshape(g * 512, n)


def gelu(v):
    return 0.5 * v * (1.0 + np.tanh(np.sqrt(2.0 / np.pi) * (v + 0.044715 * v**3)))


def bf(x):
    return np.asarray(x, np.float32).astype(ml_dtypes.bfloat16)


def planes(Y):
    n, m = Y.shape
    b = f64(bf(Y)).reshape(n // 32, 32, m)
    amax = np.abs(b).max(1)
    byte = np.clip(np.where(amax > 0, np.frexp(amax)[1] - 1 + 127 - 7, 1), 1, 254)
    codes = (b * np.exp2(127.0 - byte)[:, None, :]).reshape(n, m).astype(np.float32).astype(ml_dtypes.float8_e4m3fn).view(np.uint8)
    words = codes.reshape(n // 512, 128, 4, m).transpose(0, 1, 3, 2)
    return np.ascontiguousarray(words), np.ascontiguousarray(byte.astype(np.uint8).reshape(n // 512, 16, m))


K, T, S, H, N = 1024, 4096, 512, 1024, 512


def setup_inputs():
    n = np.random.standard_normal
    s = mx_kscale(K)[:, None]
    u = mx_kscale(H)[:, None]
    tab_words, tab_scales = pack_weight(n((K, T)) * s, "e4m3")
    w1 = 0.7 * n((K, H)) / np.sqrt(K) / s * u.T
    w2_words, w2_scales = pack_weight(0.7 * n((K, H)) / np.sqrt(K) / s * u.T, "e4m3")
    w3_words, w3_scales = pack_weight(n((K, H)) / np.sqrt(K) / s * u.T, "e2m1")
    syn = 0.7 * n((H, S)) * u
    w4 = n((H, N)) / np.sqrt(H) / u * np.exp(0.8 * n(N))
    return {
        "tab_words": tab_words, "tab_scales": tab_scales,
        "offs": striped(np.random.permutation(T)[:S]),
        "offs2": striped(np.random.permutation(T)[:S]),
        "offs3": striped(np.random.permutation(T)[:S]),
        "w1": w1.astype(np.float32),
        "w2_words": w2_words, "w2_scales": w2_scales,
        "w3_words": w3_words, "w3_scales": w3_scales,
        "syn": syn.astype(np.float32),
        "w4": w4.astype(np.float32),
    }


def reference(tab_words, tab_scales, offs, offs2, offs3, w1, w2_words, w2_scales,
              w3_words, w3_scales, syn, w4):
    TW = unpack_weight(tab_words, tab_scales, "e4m3")
    v = TW[:, unstriped(offs)]
    v2 = TW[:, unstriped(offs2)]
    v3 = TW[:, unstriped(offs3)]
    w1q = mxq(f64(w1), 0, "e4m3")
    w2 = unpack_weight(w2_words, w2_scales, "e4m3")
    w3 = unpack_weight(w3_words, w3_scales, "e2m1")
    ctx = w1q.T @ v + w2.T @ v2
    pron = w3.T @ v3
    h = np.maximum(ctx, pron) + f64(syn)
    hq = mxq(h, 0, "e4m3")
    w4q = mxq(f64(w4), 0, "e4m3")
    y = w4q.T @ hq
    words, scales = planes(y)
    return y, words, scales

@@ -1,0 +1,320 @@
+from contextlib import ExitStack
+
+import concourse.mybir as mybir
+
+K, T, S, H, N = 1024, 4096, 512, 1024, 512
+FLOPS = 2 * (3 * K * H * S + H * N * S)
+
+F32 = mybir.dt.float32
+BF16 = mybir.dt.bfloat16
+I32 = mybir.dt.int32
+U32 = mybir.dt.uint32
+U16 = mybir.dt.uint16
+U8 = mybir.dt.uint8
+E4M3 = mybir.dt.float8_e4m3fn_x4
+E2M1 = mybir.dt.float4_e2m1fn_x4
+MAX = mybir.AluOpType.max
+ADD = mybir.AluOpType.add
+
+P = 128
+PASS = 512
+HALF = S // 2
+
+
+def tile_list_homograph_context_features_kernel(
+    tc, tab_words, tab_scales, offs, offs2, offs3, w1, w2_words, w2_scales,
+    w3_words, w3_scales, syn, w4, out_0, out_1, out_2,
+):
+    nc = tc.nc
+    with ExitStack() as ctx:
+        sb = ctx.enter_context(tc.tile_pool(name="sb", bufs=1))
+        ps = ctx.enter_context(tc.psum_pool(name="ps", bufs=1))
+
+        def tile(name, shape, dtype):
+            return sb.tile(shape, dtype, name=name, align_bytes=64)
+
+        lists = [sb.tile([P, S // 16], U16, name="list%d" % l) for l in range(3)]
+        tabw = [tile("tabw%d" % a, [P, T], U32) for a in range(2)]
+        tabs = tile("tabs", [P, T], U8)
+        wsc_raw = tile("wsc_raw", [P, 2 * H], U8)
+        wsc = tile("wsc", [P, 2 * H], U8)
+        shifted = tile("shifted", [P, S], U8)
+        w1_raw = {(a, b): tile("w1raw%d%d" % (a, b), [P, 4, PASS], F32) for a in range(2) for b in range(2)}
+        w2_raw = tile("w2raw", [P, 2 * H], I32)
+        w3_raw = tile("w3raw", [P, H], I32)
+        w2_d = [tile("w2d%d" % b, [P, 2 * PASS], I32) for b in range(2)]
+        w3_d = tile("w3d", [P, 4 * H], U8)
+        w4_raw = [tile("w4raw%d" % b, [P, 4, N], F32) for b in range(2)]
+        syn_sb = [tile("syn%d" % b, [P, 4, S], F32) for b in range(2)]
+
+        nc.vector.memset(tabs[:].bitcast(I32), 0)
+        nc.vector.memset(wsc_raw[:].bitcast(I32), 0)
+        nc.vector.memset(shifted[:].bitcast(I32), 0)
+
+        for l, src in enumerate((offs, offs2, offs3)):
+            nc.sync.dma_start(lists[l][:], src)
+        tabs_i = tab_scales.bitcast(I32)
+        for q in range(4):
+            nc.gpsimd.dma_start(out=tabs[32 * q : 32 * q + 8, :].bitcast(I32), in_=tabs_i[:, 4 * q : 4 * q + 4, :])
+
+        def load_wscales(src, first):
+            rows = src.bitcast(I32).rearrange("a r c -> r a c")
+            for q in range(4):
+                nc.gpsimd.dma_start(
+                    out=wsc_raw[32 * q + first : 32 * q + first + 4, :].bitcast(I32).rearrange("p (a c) -> p a c", a=2),
+                    in_=rows[4 * q : 4 * q + 4],
+                )
+
+        load_wscales(w3_scales, 0)
+        load_wscales(w2_scales, 4)
+
+        def load_w1(a, b):
+            nc.sync.dma_start(
+                out=w1_raw[a, b][:],
+                in_=w1[PASS * a : PASS * (a + 1), PASS * b : PASS * (b + 1)].rearrange("(p i) c -> p i c", i=4),
+            )
+
+        def load_table(a):
+            nc.sync.dma_start(out=tabw[a][:].bitcast(I32), in_=tab_words[a].rearrange("p t i -> p (t i)").bitcast(I32))
+
+        def load_rows(dst, src, b, cols):
+            rows = src[PASS * b : PASS * (b + 1), :].rearrange("(q t i) c -> t q i c", t=4, i=8)
+            for t in range(4):
+                nc.sync.dma_start(out=dst[:, t, cols], in_=rows[t][:, :, cols])
+
+        load_w1(0, 0)
+        load_table(0)
+        nc.sync.dma_start(
+            out=w3_raw[:].rearrange("p (a c) -> p a c", a=2),
+            in_=w3_words.bitcast(I32).rearrange("a p c -> p a c"),
+        )
+        nc.sync.dma_start(
+            out=w2_raw[:].rearrange("p (a c) -> p a c", a=2),
+            in_=w2_words.rearrange("a p c i -> p a (c i)").bitcast(I32),
+        )
+        load_table(1)
+        load_w1(1, 0)
+        load_w1(0, 1)
+        load_w1(1, 1)
+        load_rows(syn_sb[0], syn, 0, slice(0, S))
+        load_rows(w4_raw[0], w4, 0, slice(0, N))
+        load_rows(w4_raw[1], w4, 1, slice(0, N))
+        load_rows(syn_sb[1], syn, 1, slice(0, HALF))
+        load_rows(syn_sb[1], syn, 1, slice(HALF, S))
+
+        gw = {}
+        gs = {}
+
+        def gather_scales(l):
+            gs[l] = tile("gs%d" % l, [P, S], U8)
+            nc.vector.tensor_copy(gs[l][:], tabs[:].indirect(lists[l][:]))
+
+        def gather_words(l, a):
+            gw[l, a] = tile("gw%d%d" % (l, a), [P, S], U32)
+            nc.vector.tensor_copy(gw[l, a][:], tabw[a][:].indirect(lists[l][:]))
+
+        def moving(l, a):
+            if l == 2 and a == 1:
+                return gw[l, a][:].bitcast(E4M3), shifted[:]
+            return gw[l, a][:].bitcast(E4M3), gs[l][4 * a : P, :]
+
+        w1_b, w1_q, w1_s = {}, {}, {}
+
+        def cast_w1(a, b, eng):
+            w1_b[a, b] = tile("w1b%d%d" % (a, b), [P, 4 * PASS], BF16)
+            dst = w1_b[a, b][:].rearrange("p (t q i k) -> p t q k i", t=4, q=16, i=8)
+            src = w1_raw[a, b][:].rearrange("p k (q t i) -> p t q k i", t=4, i=8)
+            if eng == "s":
+                nc.scalar.copy(dst, src)
+            else:
+                nc.vector.tensor_copy(dst, src)
+
+        def quant(name, src, width):
+            codes = tile(name + "c", [P, width], U32)
+            scales = tile(name + "s", [P, width], U8)
+            nc.vector.quantize_mx(out=codes[:].bitcast(E4M3), scales=scales[:], in_=src)
+            return codes, scales
+
+        def quant_w1(a, b):
+            w1_q[a, b], w1_s[a, b] = quant("w1q%d%d" % (a, b), w1_b[a, b][:], PASS)
+
+        w4_b, w4_q = {}, {}
+
+        def cast_w4(b):
+            w4_b[b] = tile("w4b%d" % b, [P, 4 * N], BF16)
+            nc.scalar.copy(
+                w4_b[b][:].rearrange("p (u m t) -> p m t u", u=4, t=4),
+                w4_raw[b][:].rearrange("p t (m u) -> p m t u", u=4),
+            )
+
+        def quant_w4(b):
+            w4_q[b] = quant("w4q%d" % b, w4_b[b][:], N)
+
+        def bank(tag):
+            return ps.tile([P, 512], F32, name=tag, tag=tag)
+
+        def col(a, b, t):
+            return a * H + b * PASS + t * P
+
+        def mm_pron(banks, b, a):
+            rhs, rhs_s = moving(2, a)
+            for t in range(4):
+                c = col(a, b, t)
+                nc.tensor.matmul_mx(
+                    out=banks[t][:], lhsT=w3_d[:, 2 * c : 2 * (c + P)].bitcast(E2M1), lhsT_scale=wsc[:, c : c + P],
+                    rhs=rhs, rhs_scale=rhs_s, start=(a == 0), stop=(a == 1),
+                )
+
+        def mm_w1(banks, b, a, start, stop):
+            rhs, rhs_s = moving(0, a)
+            for t in range(4):
+                nc.tensor.matmul_mx(
+                    out=banks[t][:], lhsT=w1_q[a, b][:, t * P : (t + 1) * P].bitcast(E4M3),
+                    lhsT_scale=w1_s[a, b][:, t * P : (t + 1) * P],
+                    rhs=rhs, rhs_scale=rhs_s, start=start, stop=stop,
+                )
+
+        def mm_w2(banks, b, t, a, start, stop):
+            rhs, rhs_s = moving(1, a)
+            c = col(a, b, t)
+            d = a * PASS + t * P
+            nc.tensor.matmul_mx(
+                out=banks[t][:], lhsT=w2_d[b][:, d : d + P].bitcast(E4M3), lhsT_scale=wsc[4:P, c : c + P],
+                rhs=rhs, rhs_scale=rhs_s, start=start, stop=stop,
+            )
+
+        def deal_w2(b):
+            nc.scalar.copy(
+                w2_d[b][:].bitcast(U32).rearrange("p (a t q i) -> p a t q i", a=2, t=4, i=8),
+                w2_raw[:].bitcast(U32).rearrange("p (a b q t i) -> p b a t q i", a=2, b=2, t=4, i=8)[:, b],
+            )
+
+        pron_sb, larger, h_b, h_q = {}, {}, {}, {}
+
+        def copy_pron(banks, b):
+            pron_sb[b] = tile("pron%d" % b, [P, 4, S], F32)
+            for t in range(4):
+                nc.scalar.copy(pron_sb[b][:, t, :], banks[t][:])
+
+        def take_max(banks, b):
+            larger[b] = pron_sb[b]
+            for t in range(4):
+                nc.vector.tensor_tensor(larger[b][:, t, :], banks[t][:], pron_sb[b][:, t, :], MAX)
+
+        def add_syn(b, hf):
+            cols = slice(hf * HALF, (hf + 1) * HALF)
+            h_b[b, hf] = tile("hb%d%d" % (b, hf), [P, 4 * HALF], BF16)
+            nc.vector.tensor_tensor(
+                h_b[b, hf][:].rearrange("p (c e t) -> p c t e", e=4, t=4),
+                larger[b][:, :, cols].rearrange("p t (c e) -> p c t e", e=4),
+                syn_sb[b][:, :, cols].rearrange("p t (c e) -> p c t e", e=4),
+                ADD,
+            )
+
+        def quant_h(b, hf):
+            h_q[b, hf] = quant("hq%d%d" % (b, hf), h_b[b, hf][:], HALF)
+
+        def mm_y(banks, b, hf):
+            codes, scales = w4_q[b]
+            hc, hs = h_q[b, hf]
+            for u in range(4):
+                nc.tensor.matmul_mx(
+                    out=banks[2 * hf + u // 2][:, (u % 2) * HALF : (u % 2 + 1) * HALF],
+                    lhsT=codes[:, u * P : (u + 1) * P].bitcast(E4M3), lhsT_scale=scales[:, u * P : (u + 1) * P],
+                    rhs=hc[:].bitcast(E4M3), rhs_scale=hs[:],
+                    start=(b == 0 and u % 2 == 0), stop=(b == 1 and u % 2 == 1),
+                )
+
+        gather_scales(2)
+        for q in range(4):
+            nc.gpsimd.dma_start(
+                out=shifted[32 * q : 32 * q + 4, :].bitcast(I32), in_=gs[2][32 * q + 4 : 32 * q + 8, :].bitcast(I32)
+            )
+        gather_scales(1)
+        gather_scales(0)
+        cast_w1(0, 0, "s")
+        quant_w1(0, 0)
+        for l in (0, 2, 1):
+            gather_words(l, 0)
+        nc.scalar.copy(
+            w3_d[:].bitcast(U32).rearrange("p (g t q i) -> p g t q i", t=4, q=16, i=4),
+            w3_raw[:].bitcast(U32).rearrange("p (g q t i) -> p g t q i", t=4, q=16, i=4),
+        )
+        nc.scalar.copy(
+            wsc[:].bitcast(U32).rearrange("p (g t q i) -> p g t q i", t=4, q=16, i=2),
+            wsc_raw[:].bitcast(U32).rearrange("p (g q t i) -> p g t q i", t=4, q=16, i=2),
+        )
+        deal_w2(0)
+        deal_w2(1)
+        pron0 = [bank("p%d" % t) for t in range(4)]
+        ctx0 = [bank("c%d" % t) for t in range(4)]
+        mm_w1(ctx0, 0, 0, True, False)
+        mm_pron(pron0, 0, 0)
+        for t in range(4):
+            mm_w2(ctx0, 0, t, 0, False, False)
+        for l in (2, 1, 0):
+            gather_words(l, 1)
+        mm_pron(pron0, 0, 1)
+        copy_pron(pron0, 0)
+        for t in range(4):
+            mm_w2(ctx0, 0, t, 1, False, False)
+        cast_w1(1, 0, "v")
+        quant_w1(1, 0)
+        pron1 = [bank("p%d" % t) for t in range(4)]
+        mm_pron(pron1, 1, 0)
+        mm_pron(pron1, 1, 1)
+        copy_pron(pron1, 1)
+        mm_w1(ctx0, 0, 1, False, True)
+        cast_w1(0, 1, "s")
+        cast_w1(1, 1, "s")
+        take_max(ctx0, 0)
+        ctx1 = [bank("p%d" % t) for t in range(4)]
+        for t in range(4):
+            mm_w2(ctx1, 1, t, 0, True, False)
+            mm_w2(ctx1, 1, t, 1, False, False)
+        quant_w1(0, 1)
+        mm_w1(ctx1, 1, 0, False, False)
+        add_syn(0, 0)
+        add_syn(0, 1)
+        quant_w1(1, 1)
+        mm_w1(ctx1, 1, 1, False, True)
+        cast_w4(0)
+        cast_w4(1)
+        quant_h(0, 0)
+        quant_h(0, 1)
+        take_max(ctx1, 1)
+        quant_w4(0)
+        ybanks = [bank("c%d" % t) for t in range(4)]
+        mm_y(ybanks, 0, 0)
+        mm_y(ybanks, 0, 1)
+        quant_w4(1)
+
+        y32 = [tile("y32_%d" % hf, [P, 4, HALF], F32) for hf in range(2)]
+        y_codes = tile("ycodes", [P, S], U32)
+        y_scales = tile("yscales", [P, S], U8)
+        out_rows = out_0.rearrange("(p u) j -> p u j", u=4)
+        out_words = out_1[0].rearrange("p m t -> p (m t)").bitcast(I32)
+
+        def finish(hf):
+            cols = slice(hf * HALF, (hf + 1) * HALF)
+            nc.scalar.copy(y32[hf][:, 0:2, :].rearrange("p u j -> p (u j)"), ybanks[2 * hf][:])
+            nc.vector.tensor_copy(y32[hf][:, 2:4, :].rearrange("p u j -> p (u j)"), ybanks[2 * hf + 1][:])
+            nc.sync.dma_start(out=out_rows[:, :, cols], in_=y32[hf][:])
+            y_b = tile("yb%d" % hf, [P, 4 * HALF], BF16)
+            nc.vector.tensor_copy(
+                y_b[:].rearrange("p (c e u) -> p c u e", e=4, u=4),
+                y32[hf][:].rearrange("p u (c e) -> p c u e", e=4),
+            )
+            nc.vector.quantize_mx(out=y_codes[:, cols].bitcast(E4M3), scales=y_scales[:, cols], in_=y_b[:])
+            nc.sync.dma_start(out=out_words[:, cols], in_=y_codes[:, cols].bitcast(I32))
+
+        for hf in range(2):
+            add_syn(1, hf)
+            quant_h(1, hf)
+            mm_y(ybanks, 1, hf)
+        finish(0)
+        finish(1)
+        out_scales = out_2[0].bitcast(I32)
+        for q in range(4):
+            eng = nc.sync if q % 2 == 0 else nc.scalar
+            eng.dma_start(out=out_scales[4 * q : 4 * q + 4, :], in_=y_scales[32 * q : 32 * q + 4, :].bitcast(I32))

@@ -38,7 +38,7 @@ def tile_list_homograph_context_features_kernel(
         tabs = tile("tabs", [P, T], U8)
         wsc_raw = tile("wsc_raw", [P, 2 * H], U8)
         wsc = tile("wsc", [P, 2 * H], U8)
-        shifted = tile("shifted", [P, S], U8)
+        tabs1 = tile("tabs1", [P, T], U8)
         w1_raw = {(a, b): tile("w1raw%d%d" % (a, b), [P, 4, PASS], F32) for a in range(2) for b in range(2)}
         w2_raw = tile("w2raw", [P, 2 * H], I32)
         w3_raw = tile("w3raw", [P, H], I32)
@@ -49,24 +49,28 @@ def tile_list_homograph_context_features_kernel(
 
         nc.vector.memset(tabs[:].bitcast(I32), 0)
         nc.vector.memset(wsc_raw[:].bitcast(I32), 0)
-        nc.vector.memset(shifted[:].bitcast(I32), 0)
+        nc.vector.memset(tabs1[:].bitcast(I32), 0)
 
         for l, src in enumerate((offs, offs2, offs3)):
             nc.sync.dma_start(lists[l][:], src)
         tabs_i = tab_scales.bitcast(I32)
-        for q in range(4):
-            nc.gpsimd.dma_start(out=tabs[32 * q : 32 * q + 8, :].bitcast(I32), in_=tabs_i[:, 4 * q : 4 * q + 4, :])
+
+        def load_tab_scales():
+            for q in range(4):
+                nc.sync.dma_start(out=tabs[32 * q : 32 * q + 8, :].bitcast(I32), in_=tabs_i[:, 4 * q : 4 * q + 4, :])
+
+        def load_tab_scales1():
+            for q in range(4):
+                nc.sync.dma_start(out=tabs1[32 * q : 32 * q + 4, :].bitcast(I32), in_=tabs_i[1, 4 * q : 4 * q + 4, :])
 
         def load_wscales(src, first):
             rows = src.bitcast(I32).rearrange("a r c -> r a c")
             for q in range(4):
-                nc.gpsimd.dma_start(
+                nc.sync.dma_start(
                     out=wsc_raw[32 * q + first : 32 * q + first + 4, :].bitcast(I32).rearrange("p (a c) -> p a c", a=2),
                     in_=rows[4 * q : 4 * q + 4],
                 )
 
-        load_wscales(w3_scales, 0)
-        load_wscales(w2_scales, 4)
 
         def load_w1(a, b):
             nc.sync.dma_start(
@@ -83,15 +87,19 @@ def tile_list_homograph_context_features_kernel(
                 nc.sync.dma_start(out=dst[:, t, cols], in_=rows[t][:, :, cols])
 
         load_w1(0, 0)
+        load_tab_scales()
         load_table(0)
-        nc.sync.dma_start(
-            out=w3_raw[:].rearrange("p (a c) -> p a c", a=2),
-            in_=w3_words.bitcast(I32).rearrange("a p c -> p a c"),
-        )
+        load_wscales(w3_scales, 0)
         nc.sync.dma_start(
             out=w2_raw[:].rearrange("p (a c) -> p a c", a=2),
             in_=w2_words.rearrange("a p c i -> p a (c i)").bitcast(I32),
         )
+        load_wscales(w2_scales, 4)
+        nc.sync.dma_start(
+            out=w3_raw[:].rearrange("p (a c) -> p a c", a=2),
+            in_=w3_words.bitcast(I32).rearrange("a p c -> p a c"),
+        )
+        load_tab_scales1()
         load_table(1)
         load_w1(1, 0)
         load_w1(0, 1)
@@ -104,6 +112,7 @@ def tile_list_homograph_context_features_kernel(
 
         gw = {}
         gs = {}
+        gs1 = tile("gs_second", [P, S], U8)
 
         def gather_scales(l):
             gs[l] = tile("gs%d" % l, [P, S], U8)
@@ -115,7 +124,7 @@ def tile_list_homograph_context_features_kernel(
 
         def moving(l, a):
             if l == 2 and a == 1:
-                return gw[l, a][:].bitcast(E4M3), shifted[:]
+                return gw[l, a][:].bitcast(E4M3), gs1[:]
             return gw[l, a][:].bitcast(E4M3), gs[l][4 * a : P, :]
 
         w1_b, w1_q, w1_s = {}, {}, {}
@@ -226,16 +235,13 @@ def tile_list_homograph_context_features_kernel(
                 )
 
         gather_scales(2)
-        for q in range(4):
-            nc.gpsimd.dma_start(
-                out=shifted[32 * q : 32 * q + 4, :].bitcast(I32), in_=gs[2][32 * q + 4 : 32 * q + 8, :].bitcast(I32)
-            )
         gather_scales(1)
         gather_scales(0)
         cast_w1(0, 0, "s")
         quant_w1(0, 0)
-        for l in (0, 2, 1):
+        for l in (0, 1, 2):
             gather_words(l, 0)
+        deal_w2(0)
         nc.scalar.copy(
             w3_d[:].bitcast(U32).rearrange("p (g t q i) -> p g t q i", t=4, q=16, i=4),
             w3_raw[:].bitcast(U32).rearrange("p (g q t i) -> p g t q i", t=4, q=16, i=4),
@@ -244,14 +250,14 @@ def tile_list_homograph_context_features_kernel(
             wsc[:].bitcast(U32).rearrange("p (g t q i) -> p g t q i", t=4, q=16, i=2),
             wsc_raw[:].bitcast(U32).rearrange("p (g q t i) -> p g t q i", t=4, q=16, i=2),
         )
-        deal_w2(0)
         deal_w2(1)
+        nc.vector.tensor_copy(gs1[:], tabs1[:].indirect(lists[2][:]))
         pron0 = [bank("p%d" % t) for t in range(4)]
         ctx0 = [bank("c%d" % t) for t in range(4)]
         mm_w1(ctx0, 0, 0, True, False)
-        mm_pron(pron0, 0, 0)
         for t in range(4):
             mm_w2(ctx0, 0, t, 0, False, False)
+        mm_pron(pron0, 0, 0)
         for l in (2, 1, 0):
             gather_words(l, 1)
         mm_pron(pron0, 0, 1)

@@ -38,7 +38,7 @@ def tile_list_homograph_context_features_kernel(
         tabs = tile("tabs", [P, T], U8)
         wsc_raw = tile("wsc_raw", [P, 2 * H], U8)
         wsc = tile("wsc", [P, 2 * H], U8)
-        tabs1 = tile("tabs1", [P, T], U8)
+        shifted = tile("shifted", [P, S], U8)
         w1_raw = {(a, b): tile("w1raw%d%d" % (a, b), [P, 4, PASS], F32) for a in range(2) for b in range(2)}
         w2_raw = tile("w2raw", [P, 2 * H], I32)
         w3_raw = tile("w3raw", [P, H], I32)
@@ -49,28 +49,24 @@ def tile_list_homograph_context_features_kernel(
 
         nc.vector.memset(tabs[:].bitcast(I32), 0)
         nc.vector.memset(wsc_raw[:].bitcast(I32), 0)
-        nc.vector.memset(tabs1[:].bitcast(I32), 0)
+        nc.vector.memset(shifted[:].bitcast(I32), 0)
 
         for l, src in enumerate((offs, offs2, offs3)):
             nc.sync.dma_start(lists[l][:], src)
         tabs_i = tab_scales.bitcast(I32)
-
-        def load_tab_scales():
-            for q in range(4):
-                nc.sync.dma_start(out=tabs[32 * q : 32 * q + 8, :].bitcast(I32), in_=tabs_i[:, 4 * q : 4 * q + 4, :])
-
-        def load_tab_scales1():
-            for q in range(4):
-                nc.sync.dma_start(out=tabs1[32 * q : 32 * q + 4, :].bitcast(I32), in_=tabs_i[1, 4 * q : 4 * q + 4, :])
+        for q in range(4):
+            nc.gpsimd.dma_start(out=tabs[32 * q : 32 * q + 8, :].bitcast(I32), in_=tabs_i[:, 4 * q : 4 * q + 4, :])
 
         def load_wscales(src, first):
             rows = src.bitcast(I32).rearrange("a r c -> r a c")
             for q in range(4):
-                nc.sync.dma_start(
+                nc.gpsimd.dma_start(
                     out=wsc_raw[32 * q + first : 32 * q + first + 4, :].bitcast(I32).rearrange("p (a c) -> p a c", a=2),
                     in_=rows[4 * q : 4 * q + 4],
                 )
 
+        load_wscales(w3_scales, 0)
+        load_wscales(w2_scales, 4)
 
         def load_w1(a, b):
             nc.sync.dma_start(
@@ -86,33 +82,28 @@ def tile_list_homograph_context_features_kernel(
             for t in range(4):
                 nc.sync.dma_start(out=dst[:, t, cols], in_=rows[t][:, :, cols])
 
-        load_w1(0, 0)
-        load_tab_scales()
-        load_table(0)
-        load_wscales(w3_scales, 0)
-        nc.sync.dma_start(
-            out=w2_raw[:].rearrange("p (a c) -> p a c", a=2),
-            in_=w2_words.rearrange("a p c i -> p a (c i)").bitcast(I32),
-        )
-        load_wscales(w2_scales, 4)
         nc.sync.dma_start(
             out=w3_raw[:].rearrange("p (a c) -> p a c", a=2),
             in_=w3_words.bitcast(I32).rearrange("a p c -> p a c"),
         )
-        load_tab_scales1()
+        load_table(0)
+        nc.sync.dma_start(
+            out=w2_raw[:].rearrange("p (a c) -> p a c", a=2),
+            in_=w2_words.rearrange("a p c i -> p a (c i)").bitcast(I32),
+        )
         load_table(1)
+        load_w1(0, 0)
         load_w1(1, 0)
         load_w1(0, 1)
         load_w1(1, 1)
-        load_rows(syn_sb[0], syn, 0, slice(0, S))
         load_rows(w4_raw[0], w4, 0, slice(0, N))
+        load_rows(syn_sb[0], syn, 0, slice(0, S))
         load_rows(w4_raw[1], w4, 1, slice(0, N))
         load_rows(syn_sb[1], syn, 1, slice(0, HALF))
         load_rows(syn_sb[1], syn, 1, slice(HALF, S))
 
         gw = {}
         gs = {}
-        gs1 = tile("gs_second", [P, S], U8)
 
         def gather_scales(l):
             gs[l] = tile("gs%d" % l, [P, S], U8)
@@ -124,15 +115,15 @@ def tile_list_homograph_context_features_kernel(
 
         def moving(l, a):
             if l == 2 and a == 1:
-                return gw[l, a][:].bitcast(E4M3), gs1[:]
+                return gw[l, a][:].bitcast(E4M3), shifted[:]
             return gw[l, a][:].bitcast(E4M3), gs[l][4 * a : P, :]
 
         w1_b, w1_q, w1_s = {}, {}, {}
 
         def cast_w1(a, b, eng):
             w1_b[a, b] = tile("w1b%d%d" % (a, b), [P, 4 * PASS], BF16)
-            dst = w1_b[a, b][:].rearrange("p (t q i k) -> p t q k i", t=4, q=16, i=8)
-            src = w1_raw[a, b][:].rearrange("p k (q t i) -> p t q k i", t=4, i=8)
+            dst = w1_b[a, b][:].rearrange("p (t q i k) -> p t q i k", t=4, q=16, i=8)
+            src = w1_raw[a, b][:].rearrange("p k (q t i) -> p t q i k", t=4, i=8)
             if eng == "s":
                 nc.scalar.copy(dst, src)
             else:
@@ -152,8 +143,8 @@ def tile_list_homograph_context_features_kernel(
         def cast_w4(b):
             w4_b[b] = tile("w4b%d" % b, [P, 4 * N], BF16)
             nc.scalar.copy(
-                w4_b[b][:].rearrange("p (u m t) -> p m t u", u=4, t=4),
-                w4_raw[b][:].rearrange("p t (m u) -> p m t u", u=4),
+                w4_b[b][:].rearrange("p (u m t) -> p u m t", u=4, t=4),
+                w4_raw[b][:].rearrange("p t (m u) -> p u m t", u=4),
             )
 
         def quant_w4(b):
@@ -214,9 +205,9 @@ def tile_list_homograph_context_features_kernel(
             cols = slice(hf * HALF, (hf + 1) * HALF)
             h_b[b, hf] = tile("hb%d%d" % (b, hf), [P, 4 * HALF], BF16)
             nc.vector.tensor_tensor(
-                h_b[b, hf][:].rearrange("p (c e t) -> p c t e", e=4, t=4),
-                larger[b][:, :, cols].rearrange("p t (c e) -> p c t e", e=4),
-                syn_sb[b][:, :, cols].rearrange("p t (c e) -> p c t e", e=4),
+                h_b[b, hf][:].rearrange("p (c e t) -> p c t e", e=2, t=4),
+                larger[b][:, :, cols].rearrange("p t (c e) -> p c t e", e=2),
+                syn_sb[b][:, :, cols].rearrange("p t (c e) -> p c t e", e=2),
                 ADD,
             )
 
@@ -235,65 +226,67 @@ def tile_list_homograph_context_features_kernel(
                 )
 
         gather_scales(2)
+        for q in range(4):
+            nc.gpsimd.dma_start(
+                out=shifted[32 * q : 32 * q + 4, :].bitcast(I32), in_=gs[2][32 * q + 4 : 32 * q + 8, :].bitcast(I32)
+            )
         gather_scales(1)
         gather_scales(0)
-        cast_w1(0, 0, "s")
-        quant_w1(0, 0)
-        for l in (0, 1, 2):
-            gather_words(l, 0)
-        deal_w2(0)
         nc.scalar.copy(
             w3_d[:].bitcast(U32).rearrange("p (g t q i) -> p g t q i", t=4, q=16, i=4),
             w3_raw[:].bitcast(U32).rearrange("p (g q t i) -> p g t q i", t=4, q=16, i=4),
         )
+        for l in (2, 1, 0):
+            gather_words(l, 0)
         nc.scalar.copy(
             wsc[:].bitcast(U32).rearrange("p (g t q i) -> p g t q i", t=4, q=16, i=2),
             wsc_raw[:].bitcast(U32).rearrange("p (g q t i) -> p g t q i", t=4, q=16, i=2),
         )
+        deal_w2(0)
         deal_w2(1)
-        nc.vector.tensor_copy(gs1[:], tabs1[:].indirect(lists[2][:]))
         pron0 = [bank("p%d" % t) for t in range(4)]
         ctx0 = [bank("c%d" % t) for t in range(4)]
-        mm_w1(ctx0, 0, 0, True, False)
-        for t in range(4):
-            mm_w2(ctx0, 0, t, 0, False, False)
         mm_pron(pron0, 0, 0)
+        for t in range(4):
+            mm_w2(ctx0, 0, t, 0, True, False)
         for l in (2, 1, 0):
             gather_words(l, 1)
         mm_pron(pron0, 0, 1)
         copy_pron(pron0, 0)
         for t in range(4):
             mm_w2(ctx0, 0, t, 1, False, False)
-        cast_w1(1, 0, "v")
-        quant_w1(1, 0)
         pron1 = [bank("p%d" % t) for t in range(4)]
         mm_pron(pron1, 1, 0)
         mm_pron(pron1, 1, 1)
         copy_pron(pron1, 1)
+        cast_w1(0, 0, "v")
+        quant_w1(0, 0)
+        cast_w1(1, 0, "v")
+        mm_w1(ctx0, 0, 0, False, False)
+        quant_w1(1, 0)
         mm_w1(ctx0, 0, 1, False, True)
-        cast_w1(0, 1, "s")
-        cast_w1(1, 1, "s")
-        take_max(ctx0, 0)
         ctx1 = [bank("p%d" % t) for t in range(4)]
         for t in range(4):
             mm_w2(ctx1, 1, t, 0, True, False)
             mm_w2(ctx1, 1, t, 1, False, False)
+        cast_w1(0, 1, "s")
+        take_max(ctx0, 0)
         quant_w1(0, 1)
         mm_w1(ctx1, 1, 0, False, False)
-        add_syn(0, 0)
-        add_syn(0, 1)
+        cast_w1(1, 1, "v")
         quant_w1(1, 1)
         mm_w1(ctx1, 1, 1, False, True)
         cast_w4(0)
         cast_w4(1)
+        take_max(ctx1, 1)
+        add_syn(0, 0)
+        add_syn(0, 1)
         quant_h(0, 0)
         quant_h(0, 1)
-        take_max(ctx1, 1)
         quant_w4(0)
         ybanks = [bank("c%d" % t) for t in range(4)]
         mm_y(ybanks, 0, 0)
         mm_y(ybanks, 0, 1)
-        quant_w4(1)
 
         y32 = [tile("y32_%d" % hf, [P, 4, HALF], F32) for hf in range(2)]
         y_codes = tile("ycodes", [P, S], U32)
@@ -308,16 +301,19 @@ def tile_list_homograph_context_features_kernel(
             nc.sync.dma_start(out=out_rows[:, :, cols], in_=y32[hf][:])
             y_b = tile("yb%d" % hf, [P, 4 * HALF], BF16)
             nc.vector.tensor_copy(
-                y_b[:].rearrange("p (c e u) -> p c u e", e=4, u=4),
-                y32[hf][:].rearrange("p u (c e) -> p c u e", e=4),
+                y_b[:].rearrange("p (j u) -> p j u", u=4),
+                y32[hf][:].rearrange("p u j -> p j u"),
             )
             nc.vector.quantize_mx(out=y_codes[:, cols].bitcast(E4M3), scales=y_scales[:, cols], in_=y_b[:])
             nc.sync.dma_start(out=out_words[:, cols], in_=y_codes[:, cols].bitcast(I32))
 
-        for hf in range(2):
-            add_syn(1, hf)
-            quant_h(1, hf)
-            mm_y(ybanks, 1, hf)
+        add_syn(1, 0)
+        quant_w4(1)
+        quant_h(1, 0)
+        mm_y(ybanks, 1, 0)
+        add_syn(1, 1)
+        quant_h(1, 1)
+        mm_y(ybanks, 1, 1)
         finish(0)
         finish(1)
         out_scales = out_2[0].bitcast(I32)

@@ -35,10 +35,9 @@ def tile_list_homograph_context_features_kernel(
 
         lists = [sb.tile([P, S // 16], U16, name="list%d" % l) for l in range(3)]
         tabw = [tile("tabw%d" % a, [P, T], U32) for a in range(2)]
-        tabs = tile("tabs", [P, T], U8)
+        tabs = tile("tabs", [P, 2 * T], U8)
         wsc_raw = tile("wsc_raw", [P, 2 * H], U8)
         wsc = tile("wsc", [P, 2 * H], U8)
-        shifted = tile("shifted", [P, S], U8)
         w1_raw = {(a, b): tile("w1raw%d%d" % (a, b), [P, 4, PASS], F32) for a in range(2) for b in range(2)}
         w2_raw = tile("w2raw", [P, 2 * H], I32)
         w3_raw = tile("w3raw", [P, H], I32)
@@ -48,25 +47,17 @@ def tile_list_homograph_context_features_kernel(
         syn_sb = [tile("syn%d" % b, [P, 4, S], F32) for b in range(2)]
 
         nc.vector.memset(tabs[:].bitcast(I32), 0)
-        nc.vector.memset(wsc_raw[:].bitcast(I32), 0)
-        nc.vector.memset(shifted[:].bitcast(I32), 0)
+        nc.gpsimd.memset(wsc_raw[:].bitcast(I32), 0)
 
         for l, src in enumerate((offs, offs2, offs3)):
             nc.sync.dma_start(lists[l][:], src)
-        tabs_i = tab_scales.bitcast(I32)
-        for q in range(4):
-            nc.gpsimd.dma_start(out=tabs[32 * q : 32 * q + 8, :].bitcast(I32), in_=tabs_i[:, 4 * q : 4 * q + 4, :])
 
-        def load_wscales(src, first):
-            rows = src.bitcast(I32).rearrange("a r c -> r a c")
-            for q in range(4):
-                nc.gpsimd.dma_start(
-                    out=wsc_raw[32 * q + first : 32 * q + first + 4, :].bitcast(I32).rearrange("p (a c) -> p a c", a=2),
-                    in_=rows[4 * q : 4 * q + 4],
+        def load_scale_rows(dst, src, first):
+            rows = src.bitcast(I32).rearrange("a (q r) c -> r q a c", r=4)
+            for r in range(4):
+                nc.sync.dma_start(
+                    out=dst[first + r : P : 32, :].bitcast(I32).rearrange("q (a c) -> q a c", a=2), in_=rows[r]
                 )
-
-        load_wscales(w3_scales, 0)
-        load_wscales(w2_scales, 4)
 
         def load_w1(a, b):
             nc.sync.dma_start(
@@ -86,6 +77,9 @@ def tile_list_homograph_context_features_kernel(
             out=w3_raw[:].rearrange("p (a c) -> p a c", a=2),
             in_=w3_words.bitcast(I32).rearrange("a p c -> p a c"),
         )
+        load_scale_rows(wsc_raw, w3_scales, 0)
+        load_scale_rows(wsc_raw, w2_scales, 4)
+        load_scale_rows(tabs, tab_scales, 0)
         load_table(0)
         nc.sync.dma_start(
             out=w2_raw[:].rearrange("p (a c) -> p a c", a=2),
@@ -105,18 +99,16 @@ def tile_list_homograph_context_features_kernel(
         gw = {}
         gs = {}
 
-        def gather_scales(l):
-            gs[l] = tile("gs%d" % l, [P, S], U8)
-            nc.vector.tensor_copy(gs[l][:], tabs[:].indirect(lists[l][:]))
+        def gather_scales(l, a):
+            gs[l, a] = tile("gs%d%d" % (l, a), [P, S], U8)
+            nc.vector.tensor_copy(gs[l, a][:], tabs[:, a * T : (a + 1) * T].indirect(lists[l][:]))
 
         def gather_words(l, a):
             gw[l, a] = tile("gw%d%d" % (l, a), [P, S], U32)
             nc.vector.tensor_copy(gw[l, a][:], tabw[a][:].indirect(lists[l][:]))
 
         def moving(l, a):
-            if l == 2 and a == 1:
-                return gw[l, a][:].bitcast(E4M3), shifted[:]
-            return gw[l, a][:].bitcast(E4M3), gs[l][4 * a : P, :]
+            return gw[l, a][:].bitcast(E4M3), gs[l, a][:]
 
         w1_b, w1_q, w1_s = {}, {}, {}
 
@@ -225,19 +217,16 @@ def tile_list_homograph_context_features_kernel(
                     start=(b == 0 and u % 2 == 0), stop=(b == 1 and u % 2 == 1),
                 )
 
-        gather_scales(2)
-        for q in range(4):
-            nc.gpsimd.dma_start(
-                out=shifted[32 * q : 32 * q + 4, :].bitcast(I32), in_=gs[2][32 * q + 4 : 32 * q + 8, :].bitcast(I32)
-            )
-        gather_scales(1)
-        gather_scales(0)
+        for l in (2, 1, 0):
+            gather_scales(l, 0)
         nc.scalar.copy(
             w3_d[:].bitcast(U32).rearrange("p (g t q i) -> p g t q i", t=4, q=16, i=4),
             w3_raw[:].bitcast(U32).rearrange("p (g q t i) -> p g t q i", t=4, q=16, i=4),
         )
         for l in (2, 1, 0):
             gather_words(l, 0)
+        for l in (2, 1, 0):
+            gather_scales(l, 1)
         nc.scalar.copy(
             wsc[:].bitcast(U32).rearrange("p (g t q i) -> p g t q i", t=4, q=16, i=2),
             wsc_raw[:].bitcast(U32).rearrange("p (g q t i) -> p g t q i", t=4, q=16, i=2),

@@ -1,6 +1,7 @@
 from contextlib import ExitStack
 
 import concourse.mybir as mybir
+from concourse.masks import make_identity
 
 K, T, S, H, N = 1024, 4096, 512, 1024, 512
 FLOPS = 2 * (3 * K * H * S + H * N * S)
@@ -17,8 +18,13 @@ MAX = mybir.AluOpType.max
 ADD = mybir.AluOpType.add
 
 P = 128
-PASS = 512
+PACK = 4
+PASS = P * PACK
+QUAD = 32
+GROUPS = S // P
 HALF = S // 2
+W2_ROW = 4
+BY_W1, BY_W2, BY_W3 = 0, 1, 2
 
 
 def tile_list_homograph_context_features_kernel(
@@ -26,286 +32,258 @@ def tile_list_homograph_context_features_kernel(
     w3_words, w3_scales, syn, w4, out_0, out_1, out_2,
 ):
     nc = tc.nc
-    with ExitStack() as ctx:
-        sb = ctx.enter_context(tc.tile_pool(name="sb", bufs=1))
-        ps = ctx.enter_context(tc.psum_pool(name="ps", bufs=1))
+    with ExitStack() as stack:
+        sb = stack.enter_context(tc.tile_pool(name="sb", bufs=1))
+        ps = stack.enter_context(tc.psum_pool(name="ps", bufs=1))
 
         def tile(name, shape, dtype):
             return sb.tile(shape, dtype, name=name, align_bytes=64)
 
+        def four_banks(tag):
+            return [ps.tile([P, PASS], F32, name="%s%d" % (tag, g), tag="%s%d" % (tag, g)) for g in range(GROUPS)]
+
         lists = [sb.tile([P, S // 16], U16, name="list%d" % l) for l in range(3)]
-        tabw = [tile("tabw%d" % a, [P, T], U32) for a in range(2)]
-        tabs = tile("tabs", [P, 2 * T], U8)
-        wsc_raw = tile("wsc_raw", [P, 2 * H], U8)
-        wsc = tile("wsc", [P, 2 * H], U8)
-        w1_raw = {(a, b): tile("w1raw%d%d" % (a, b), [P, 4, PASS], F32) for a in range(2) for b in range(2)}
-        w2_raw = tile("w2raw", [P, 2 * H], I32)
-        w3_raw = tile("w3raw", [P, H], I32)
-        w2_d = [tile("w2d%d" % b, [P, 2 * PASS], I32) for b in range(2)]
-        w3_d = tile("w3d", [P, 4 * H], U8)
-        w4_raw = [tile("w4raw%d" % b, [P, 4, N], F32) for b in range(2)]
-        syn_sb = [tile("syn%d" % b, [P, 4, S], F32) for b in range(2)]
+        table_words = [tile("table_words%d" % a, [P, T], U32) for a in range(2)]
+        table_scales = tile("table_scales", [P, 2 * T], U8)
+        weight_scales = tile("weight_scales", [P, 2 * H], U8)
+        identity = tile("identity", [P, P], F32)
+        w1_raw = {(a, b): tile("w1_raw%d%d" % (a, b), [P, PACK, PASS], F32) for a in range(2) for b in range(2)}
+        w2_codes = tile("w2_codes", [P, 2 * H], I32)
+        w3_codes = tile("w3_codes", [P, 4 * H], U8)
+        w4_raw = [tile("w4_raw%d" % b, [P, PACK, N], F32) for b in range(2)]
+        syn_sb = [tile("syn%d" % b, [P, PACK, S], F32) for b in range(2)]
 
-        nc.vector.memset(tabs[:].bitcast(I32), 0)
-        nc.gpsimd.memset(wsc_raw[:].bitcast(I32), 0)
+        nc.vector.memset(table_scales[:].bitcast(I32), 0)
+        nc.gpsimd.memset(weight_scales[:].bitcast(I32), 0)
+        make_identity(nc, identity[:])
 
-        for l, src in enumerate((offs, offs2, offs3)):
-            nc.sync.dma_start(lists[l][:], src)
 
         def load_scale_rows(dst, src, first):
             rows = src.bitcast(I32).rearrange("a (q r) c -> r q a c", r=4)
             for r in range(4):
                 nc.sync.dma_start(
-                    out=dst[first + r : P : 32, :].bitcast(I32).rearrange("q (a c) -> q a c", a=2), in_=rows[r]
+                    out=dst[first + r : P : QUAD, :].bitcast(I32).rearrange("q (a c) -> q a c", a=2), in_=rows[r]
                 )
 
         def load_w1(a, b):
             nc.sync.dma_start(
                 out=w1_raw[a, b][:],
-                in_=w1[PASS * a : PASS * (a + 1), PASS * b : PASS * (b + 1)].rearrange("(p i) c -> p i c", i=4),
+                in_=w1[PASS * a : PASS * (a + 1), PASS * b : PASS * (b + 1)].rearrange("(p i) c -> p i c", i=PACK),
             )
 
         def load_table(a):
-            nc.sync.dma_start(out=tabw[a][:].bitcast(I32), in_=tab_words[a].rearrange("p t i -> p (t i)").bitcast(I32))
+            nc.sync.dma_start(
+                out=table_words[a][:].bitcast(I32), in_=tab_words[a].rearrange("p t i -> p (t i)").bitcast(I32)
+            )
 
         def load_rows(dst, src, b, cols):
-            rows = src[PASS * b : PASS * (b + 1), :].rearrange("(q t i) c -> t q i c", t=4, i=8)
-            for t in range(4):
-                nc.sync.dma_start(out=dst[:, t, cols], in_=rows[t][:, :, cols])
+            rows = src[PASS * b : PASS * (b + 1), :].rearrange("(p t) c -> p t c", t=PACK)
+            nc.sync.dma_start(out=dst[:, :, cols], in_=rows[:, :, cols])
 
+        for l, src in enumerate((offs, offs2, offs3)):
+            nc.sync.dma_start(lists[l][:], src)
         nc.sync.dma_start(
-            out=w3_raw[:].rearrange("p (a c) -> p a c", a=2),
+            out=w3_codes[:].bitcast(I32).rearrange("p (a c) -> p a c", a=2),
             in_=w3_words.bitcast(I32).rearrange("a p c -> p a c"),
         )
-        load_scale_rows(wsc_raw, w3_scales, 0)
-        load_scale_rows(wsc_raw, w2_scales, 4)
-        load_scale_rows(tabs, tab_scales, 0)
+        load_scale_rows(weight_scales, w3_scales, 0)
+        load_scale_rows(weight_scales, w2_scales, W2_ROW)
+        load_scale_rows(table_scales, tab_scales, 0)
         load_table(0)
         nc.sync.dma_start(
-            out=w2_raw[:].rearrange("p (a c) -> p a c", a=2),
+            out=w2_codes[:].rearrange("p (a c) -> p a c", a=2),
             in_=w2_words.rearrange("a p c i -> p a (c i)").bitcast(I32),
         )
         load_table(1)
-        load_w1(0, 0)
-        load_w1(1, 0)
-        load_w1(0, 1)
-        load_w1(1, 1)
+        for b in range(2):
+            for a in range(2):
+                load_w1(a, b)
         load_rows(w4_raw[0], w4, 0, slice(0, N))
         load_rows(syn_sb[0], syn, 0, slice(0, S))
         load_rows(w4_raw[1], w4, 1, slice(0, N))
         load_rows(syn_sb[1], syn, 1, slice(0, HALF))
         load_rows(syn_sb[1], syn, 1, slice(HALF, S))
 
-        gw = {}
-        gs = {}
 
-        def gather_scales(l, a):
-            gs[l, a] = tile("gs%d%d" % (l, a), [P, S], U8)
-            nc.vector.tensor_copy(gs[l, a][:], tabs[:, a * T : (a + 1) * T].indirect(lists[l][:]))
+        picked_words, picked_scales = {}, {}
+        w1_q, w4_bf16, w4_q, h_bf16, h_q = {}, {}, {}, {}, {}
+        larger, turned = {}, {}
+        gather_order = (BY_W3, BY_W2, BY_W1)
 
-        def gather_words(l, a):
-            gw[l, a] = tile("gw%d%d" % (l, a), [P, S], U32)
-            nc.vector.tensor_copy(gw[l, a][:], tabw[a][:].indirect(lists[l][:]))
+        def gather_scales(a):
+            for l in gather_order:
+                picked_scales[l, a] = tile("picked_scales%d%d" % (l, a), [P, S], U8)
+                nc.vector.tensor_copy(picked_scales[l, a][:], table_scales[:, a * T : (a + 1) * T].indirect(lists[l][:]))
 
-        def moving(l, a):
-            return gw[l, a][:].bitcast(E4M3), gs[l, a][:]
+        def gather_words(a):
+            for l in gather_order:
+                picked_words[l, a] = tile("picked_words%d%d" % (l, a), [P, S], U32)
+                nc.vector.tensor_copy(picked_words[l, a][:], table_words[a][:].indirect(lists[l][:]))
 
-        w1_b, w1_q, w1_s = {}, {}, {}
-
-        def cast_w1(a, b, eng):
-            w1_b[a, b] = tile("w1b%d%d" % (a, b), [P, 4 * PASS], BF16)
-            dst = w1_b[a, b][:].rearrange("p (t q i k) -> p t q i k", t=4, q=16, i=8)
-            src = w1_raw[a, b][:].rearrange("p k (q t i) -> p t q i k", t=4, i=8)
-            if eng == "s":
-                nc.scalar.copy(dst, src)
-            else:
-                nc.vector.tensor_copy(dst, src)
-
-        def quant(name, src, width):
-            codes = tile(name + "c", [P, width], U32)
-            scales = tile(name + "s", [P, width], U8)
-            nc.vector.quantize_mx(out=codes[:].bitcast(E4M3), scales=scales[:], in_=src)
+        def quantise(name, src, width):
+            codes = tile(name + "_codes", [P, width], U32)
+            scales = tile(name + "_scales", [P, width], U8)
+            nc.vector.quantize_mx(out=codes[:].bitcast(E4M3), scales=scales[:], in_=src[:])
             return codes, scales
 
-        def quant_w1(a, b):
-            w1_q[a, b], w1_s[a, b] = quant("w1q%d%d" % (a, b), w1_b[a, b][:], PASS)
+        def round_w1(a, b, copy):
+            rounded = tile("w1_bf16_%d%d" % (a, b), [P, PACK * PASS], BF16)
+            copy(rounded[:].rearrange("p (c i) -> p c i", i=PACK), w1_raw[a, b][:].rearrange("p i c -> p c i"))
+            return rounded
 
-        w4_b, w4_q = {}, {}
+        def quantise_w1(a, b, rounded):
+            w1_q[a, b] = quantise("w1_%d%d" % (a, b), rounded, PASS)
 
-        def cast_w4(b):
-            w4_b[b] = tile("w4b%d" % b, [P, 4 * N], BF16)
+        def round_w4(b):
+            w4_bf16[b] = tile("w4_bf16_%d" % b, [P, PACK * N], BF16)
             nc.scalar.copy(
-                w4_b[b][:].rearrange("p (u m t) -> p u m t", u=4, t=4),
-                w4_raw[b][:].rearrange("p t (m u) -> p u m t", u=4),
+                w4_bf16[b][:].rearrange("p (u m t) -> p u m t", u=PACK, t=PACK),
+                w4_raw[b][:].rearrange("p t (m u) -> p u m t", u=PACK),
             )
 
-        def quant_w4(b):
-            w4_q[b] = quant("w4q%d" % b, w4_b[b][:], N)
+        def quantise_w4(b):
+            w4_q[b] = quantise("w4_%d" % b, w4_bf16[b], N)
 
-        def bank(tag):
-            return ps.tile([P, 512], F32, name=tag, tag=tag)
-
-        def col(a, b, t):
-            return a * H + b * PASS + t * P
-
-        def mm_pron(banks, b, a):
-            rhs, rhs_s = moving(2, a)
-            for t in range(4):
-                c = col(a, b, t)
-                nc.tensor.matmul_mx(
-                    out=banks[t][:], lhsT=w3_d[:, 2 * c : 2 * (c + P)].bitcast(E2M1), lhsT_scale=wsc[:, c : c + P],
-                    rhs=rhs, rhs_scale=rhs_s, start=(a == 0), stop=(a == 1),
-                )
-
-        def mm_w1(banks, b, a, start, stop):
-            rhs, rhs_s = moving(0, a)
-            for t in range(4):
-                nc.tensor.matmul_mx(
-                    out=banks[t][:], lhsT=w1_q[a, b][:, t * P : (t + 1) * P].bitcast(E4M3),
-                    lhsT_scale=w1_s[a, b][:, t * P : (t + 1) * P],
-                    rhs=rhs, rhs_scale=rhs_s, start=start, stop=stop,
-                )
-
-        def mm_w2(banks, b, t, a, start, stop):
-            rhs, rhs_s = moving(1, a)
-            c = col(a, b, t)
-            d = a * PASS + t * P
+        def first_stage_pass(bank, l, a, g, codes, scales, start, stop):
+            cols = slice(g * P, (g + 1) * P)
             nc.tensor.matmul_mx(
-                out=banks[t][:], lhsT=w2_d[b][:, d : d + P].bitcast(E4M3), lhsT_scale=wsc[4:P, c : c + P],
-                rhs=rhs, rhs_scale=rhs_s, start=start, stop=stop,
+                out=bank[:], lhsT=picked_words[l, a][:, cols].bitcast(E4M3), lhsT_scale=picked_scales[l, a][:, cols],
+                rhs=codes, rhs_scale=scales, start=start, stop=stop,
             )
 
-        def deal_w2(b):
-            nc.scalar.copy(
-                w2_d[b][:].bitcast(U32).rearrange("p (a t q i) -> p a t q i", a=2, t=4, i=8),
-                w2_raw[:].bitcast(U32).rearrange("p (a b q t i) -> p b a t q i", a=2, b=2, t=4, i=8)[:, b],
-            )
+        def times_w3(banks, b, a):
+            c = a * H + b * PASS
+            codes = w3_codes[:, 2 * c : 2 * (c + PASS)].bitcast(E2M1)
+            for g in range(GROUPS):
+                first_stage_pass(banks[g], BY_W3, a, g, codes, weight_scales[:, c : c + PASS], a == 0, a == 1)
 
-        pron_sb, larger, h_b, h_q = {}, {}, {}, {}
+        def times_w2(bank, b, a, g):
+            c = a * H + b * PASS
+            codes = w2_codes[:, c : c + PASS].bitcast(E4M3)
+            first_stage_pass(bank, BY_W2, a, g, codes, weight_scales[W2_ROW:P, c : c + PASS], a == 0, False)
+
+        def times_w1(banks, b, a):
+            codes, scales = w1_q[a, b]
+            for g in range(GROUPS):
+                first_stage_pass(banks[g], BY_W1, a, g, codes[:].bitcast(E4M3), scales[:], False, a == 1)
+
+        def dealt(bank):
+            return bank[:].rearrange("j (p t) -> j t p", t=PACK)
 
         def copy_pron(banks, b):
-            pron_sb[b] = tile("pron%d" % b, [P, 4, S], F32)
-            for t in range(4):
-                nc.scalar.copy(pron_sb[b][:, t, :], banks[t][:])
+            for g in range(GROUPS):
+                larger[b, g] = tile("larger%d%d" % (b, g), [P, PACK, P], F32)
+                nc.scalar.copy(larger[b, g][:], dealt(banks[g]))
 
-        def take_max(banks, b):
-            larger[b] = pron_sb[b]
-            for t in range(4):
-                nc.vector.tensor_tensor(larger[b][:, t, :], banks[t][:], pron_sb[b][:, t, :], MAX)
+        def max_and_turn(banks, b, tag):
+            for g in range(GROUPS):
+                nc.vector.tensor_tensor(larger[b, g][:], dealt(banks[g]), larger[b, g][:], MAX)
+            for g, bank in enumerate(four_banks(tag)):
+                turned[b, g] = bank
+                for t in range(PACK):
+                    nc.tensor.transpose(bank[:, t * P : (t + 1) * P], larger[b, g][:, t, :], identity[:])
 
-        def add_syn(b, hf):
-            cols = slice(hf * HALF, (hf + 1) * HALF)
-            h_b[b, hf] = tile("hb%d%d" % (b, hf), [P, 4 * HALF], BF16)
-            nc.vector.tensor_tensor(
-                h_b[b, hf][:].rearrange("p (c e t) -> p c t e", e=2, t=4),
-                larger[b][:, :, cols].rearrange("p t (c e) -> p c t e", e=2),
-                syn_sb[b][:, :, cols].rearrange("p t (c e) -> p c t e", e=2),
-                ADD,
-            )
+        def add_syn(b, half):
+            h_bf16[b, half] = tile("h_bf16_%d%d" % (b, half), [P, PACK * HALF], BF16)
+            for e in range(GROUPS // 2):
+                g = GROUPS // 2 * half + e
+                nc.vector.tensor_tensor(
+                    h_bf16[b, half][:, e * PACK * P : (e + 1) * PACK * P].rearrange("p (j t) -> p j t", t=PACK),
+                    turned[b, g][:].rearrange("p (t j) -> p j t", t=PACK),
+                    syn_sb[b][:, :, g * P : (g + 1) * P].rearrange("p t j -> p j t"),
+                    ADD,
+                )
 
-        def quant_h(b, hf):
-            h_q[b, hf] = quant("hq%d%d" % (b, hf), h_b[b, hf][:], HALF)
+        def quantise_h(b, half):
+            h_q[b, half] = quantise("h_%d%d" % (b, half), h_bf16[b, half], HALF)
 
-        def mm_y(banks, b, hf):
-            codes, scales = w4_q[b]
-            hc, hs = h_q[b, hf]
-            for u in range(4):
+        def times_w4(banks, b, half):
+            w_codes, w_scales = w4_q[b]
+            h_codes, h_scales = h_q[b, half]
+            for u in range(PACK):
                 nc.tensor.matmul_mx(
-                    out=banks[2 * hf + u // 2][:, (u % 2) * HALF : (u % 2 + 1) * HALF],
-                    lhsT=codes[:, u * P : (u + 1) * P].bitcast(E4M3), lhsT_scale=scales[:, u * P : (u + 1) * P],
-                    rhs=hc[:].bitcast(E4M3), rhs_scale=hs[:],
+                    out=banks[2 * half + u // 2][:, (u % 2) * HALF : (u % 2 + 1) * HALF],
+                    lhsT=w_codes[:, u * P : (u + 1) * P].bitcast(E4M3), lhsT_scale=w_scales[:, u * P : (u + 1) * P],
+                    rhs=h_codes[:].bitcast(E4M3), rhs_scale=h_scales[:],
                     start=(b == 0 and u % 2 == 0), stop=(b == 1 and u % 2 == 1),
                 )
 
-        for l in (2, 1, 0):
-            gather_scales(l, 0)
-        nc.scalar.copy(
-            w3_d[:].bitcast(U32).rearrange("p (g t q i) -> p g t q i", t=4, q=16, i=4),
-            w3_raw[:].bitcast(U32).rearrange("p (g q t i) -> p g t q i", t=4, q=16, i=4),
-        )
-        for l in (2, 1, 0):
-            gather_words(l, 0)
-        for l in (2, 1, 0):
-            gather_scales(l, 1)
-        nc.scalar.copy(
-            wsc[:].bitcast(U32).rearrange("p (g t q i) -> p g t q i", t=4, q=16, i=2),
-            wsc_raw[:].bitcast(U32).rearrange("p (g q t i) -> p g t q i", t=4, q=16, i=2),
-        )
-        deal_w2(0)
-        deal_w2(1)
-        pron0 = [bank("p%d" % t) for t in range(4)]
-        ctx0 = [bank("c%d" % t) for t in range(4)]
-        mm_pron(pron0, 0, 0)
-        for t in range(4):
-            mm_w2(ctx0, 0, t, 0, True, False)
-        for l in (2, 1, 0):
-            gather_words(l, 1)
-        mm_pron(pron0, 0, 1)
+
+        gather_scales(0)
+        gather_words(0)
+        gather_scales(1)
+        pron0, ctx0 = four_banks("p"), four_banks("c")
+        times_w3(pron0, 0, 0)
+        for g in range(GROUPS):
+            times_w2(ctx0[g], 0, 0, g)
+        gather_words(1)
+        times_w3(pron0, 0, 1)
         copy_pron(pron0, 0)
-        for t in range(4):
-            mm_w2(ctx0, 0, t, 1, False, False)
-        pron1 = [bank("p%d" % t) for t in range(4)]
-        mm_pron(pron1, 1, 0)
-        mm_pron(pron1, 1, 1)
+        for g in range(GROUPS):
+            times_w2(ctx0[g], 0, 1, g)
+        pron1 = four_banks("p")
+        times_w3(pron1, 1, 0)
+        times_w3(pron1, 1, 1)
         copy_pron(pron1, 1)
-        cast_w1(0, 0, "v")
-        quant_w1(0, 0)
-        cast_w1(1, 0, "v")
-        mm_w1(ctx0, 0, 0, False, False)
-        quant_w1(1, 0)
-        mm_w1(ctx0, 0, 1, False, True)
-        ctx1 = [bank("p%d" % t) for t in range(4)]
-        for t in range(4):
-            mm_w2(ctx1, 1, t, 0, True, False)
-            mm_w2(ctx1, 1, t, 1, False, False)
-        cast_w1(0, 1, "s")
-        take_max(ctx0, 0)
-        quant_w1(0, 1)
-        mm_w1(ctx1, 1, 0, False, False)
-        cast_w1(1, 1, "v")
-        quant_w1(1, 1)
-        mm_w1(ctx1, 1, 1, False, True)
-        cast_w4(0)
-        cast_w4(1)
-        take_max(ctx1, 1)
-        add_syn(0, 0)
-        add_syn(0, 1)
-        quant_h(0, 0)
-        quant_h(0, 1)
-        quant_w4(0)
-        ybanks = [bank("c%d" % t) for t in range(4)]
-        mm_y(ybanks, 0, 0)
-        mm_y(ybanks, 0, 1)
+        quantise_w1(0, 0, round_w1(0, 0, nc.vector.tensor_copy))
+        rounded = round_w1(1, 0, nc.vector.tensor_copy)
+        times_w1(ctx0, 0, 0)
+        quantise_w1(1, 0, rounded)
+        times_w1(ctx0, 0, 1)
+        ctx1 = four_banks("p")
+        for g in range(GROUPS):
+            for a in range(2):
+                times_w2(ctx1[g], 1, a, g)
+        rounded = round_w1(0, 1, nc.scalar.copy)
+        max_and_turn(ctx0, 0, "c")
+        quantise_w1(0, 1, rounded)
+        times_w1(ctx1, 1, 0)
+        quantise_w1(1, 1, round_w1(1, 1, nc.scalar.copy))
+        times_w1(ctx1, 1, 1)
+        round_w4(0)
+        round_w4(1)
+        max_and_turn(ctx1, 1, "p")
 
-        y32 = [tile("y32_%d" % hf, [P, 4, HALF], F32) for hf in range(2)]
-        y_codes = tile("ycodes", [P, S], U32)
-        y_scales = tile("yscales", [P, S], U8)
-        out_rows = out_0.rearrange("(p u) j -> p u j", u=4)
+
+        for half in range(2):
+            add_syn(0, half)
+        for half in range(2):
+            quantise_h(0, half)
+        quantise_w4(0)
+        y_banks = four_banks("c")
+        for half in range(2):
+            times_w4(y_banks, 0, half)
+
+        y = [tile("y%d" % half, [P, PACK, HALF], F32) for half in range(2)]
+        y_codes = tile("y_codes", [P, S], U32)
+        y_scales = tile("y_scales", [P, S], U8)
+        out_rows = out_0.rearrange("(p u) j -> p u j", u=PACK)
         out_words = out_1[0].rearrange("p m t -> p (m t)").bitcast(I32)
+        out_scales = out_2[0].bitcast(I32)
 
-        def finish(hf):
-            cols = slice(hf * HALF, (hf + 1) * HALF)
-            nc.scalar.copy(y32[hf][:, 0:2, :].rearrange("p u j -> p (u j)"), ybanks[2 * hf][:])
-            nc.vector.tensor_copy(y32[hf][:, 2:4, :].rearrange("p u j -> p (u j)"), ybanks[2 * hf + 1][:])
-            nc.sync.dma_start(out=out_rows[:, :, cols], in_=y32[hf][:])
-            y_b = tile("yb%d" % hf, [P, 4 * HALF], BF16)
+        def hand_out(half, second_copy):
+            cols = slice(half * HALF, (half + 1) * HALF)
+            nc.scalar.copy(y[half][:, 0:2, :].rearrange("p u j -> p (u j)"), y_banks[2 * half][:])
+            second_copy(y[half][:, 2:4, :].rearrange("p u j -> p (u j)"), y_banks[2 * half + 1][:])
+            nc.sync.dma_start(out=out_rows[:, :, cols], in_=y[half][:])
+            y_bf16 = tile("y_bf16_%d" % half, [P, PACK * HALF], BF16)
             nc.vector.tensor_copy(
-                y_b[:].rearrange("p (j u) -> p j u", u=4),
-                y32[hf][:].rearrange("p u j -> p j u"),
+                y_bf16[:].rearrange("p (j u) -> p j u", u=PACK), y[half][:].rearrange("p u j -> p j u")
             )
-            nc.vector.quantize_mx(out=y_codes[:, cols].bitcast(E4M3), scales=y_scales[:, cols], in_=y_b[:])
+            nc.vector.quantize_mx(out=y_codes[:, cols].bitcast(E4M3), scales=y_scales[:, cols], in_=y_bf16[:])
             nc.sync.dma_start(out=out_words[:, cols], in_=y_codes[:, cols].bitcast(I32))
 
         add_syn(1, 0)
-        quant_w4(1)
-        quant_h(1, 0)
-        mm_y(ybanks, 1, 0)
+        quantise_w4(1)
+        quantise_h(1, 0)
+        times_w4(y_banks, 1, 0)
         add_syn(1, 1)
-        quant_h(1, 1)
-        mm_y(ybanks, 1, 1)
-        finish(0)
-        finish(1)
-        out_scales = out_2[0].bitcast(I32)
+        quantise_h(1, 1)
+        times_w4(y_banks, 1, 1)
+        hand_out(0, nc.scalar.copy)
+        hand_out(1, nc.vector.tensor_copy)
         for q in range(4):
-            eng = nc.sync if q % 2 == 0 else nc.scalar
-            eng.dma_start(out=out_scales[4 * q : 4 * q + 4, :], in_=y_scales[32 * q : 32 * q + 4, :].bitcast(I32))
+            queue = nc.sync if q % 2 == 0 else nc.scalar
+            queue.dma_start(
+                out=out_scales[4 * q : 4 * q + 4, :], in_=y_scales[QUAD * q : QUAD * q + 4, :].bitcast(I32)
+            )

from contextlib import ExitStack

import concourse.mybir as mybir
from concourse.masks import make_identity

K, T, S, H, N = 1024, 4096, 512, 1024, 512
FLOPS = 2 * (3 * K * H * S + H * N * S)

F32 = mybir.dt.float32
BF16 = mybir.dt.bfloat16
I32 = mybir.dt.int32
U32 = mybir.dt.uint32
U16 = mybir.dt.uint16
U8 = mybir.dt.uint8
E4M3 = mybir.dt.float8_e4m3fn_x4
E2M1 = mybir.dt.float4_e2m1fn_x4
MAX = mybir.AluOpType.max
ADD = mybir.AluOpType.add

P = 128
PACK = 4
PASS = P * PACK
QUAD = 32
GROUPS = S // P
HALF = S // 2
W2_ROW = 4
BY_W1, BY_W2, BY_W3 = 0, 1, 2


def tile_list_homograph_context_features_kernel(
    tc, tab_words, tab_scales, offs, offs2, offs3, w1, w2_words, w2_scales,
    w3_words, w3_scales, syn, w4, out_0, out_1, out_2,
):
    nc = tc.nc
    with ExitStack() as stack:
        sb = stack.enter_context(tc.tile_pool(name="sb", bufs=1))
        ps = stack.enter_context(tc.psum_pool(name="ps", bufs=1))

        def tile(name, shape, dtype):
            return sb.tile(shape, dtype, name=name, align_bytes=64)

        def four_banks(tag):
            return [ps.tile([P, PASS], F32, name="%s%d" % (tag, g), tag="%s%d" % (tag, g)) for g in range(GROUPS)]

        lists = [sb.tile([P, S // 16], U16, name="list%d" % l) for l in range(3)]
        table_words = [tile("table_words%d" % a, [P, T], U32) for a in range(2)]
        table_scales = tile("table_scales", [P, 2 * T], U8)
        weight_scales = tile("weight_scales", [P, 2 * H], U8)
        identity = tile("identity", [P, P], F32)
        w1_raw = {(a, b): tile("w1_raw%d%d" % (a, b), [P, PACK, PASS], F32) for a in range(2) for b in range(2)}
        w2_codes = tile("w2_codes", [P, 2 * H], I32)
        w3_codes = tile("w3_codes", [P, 4 * H], U8)
        w4_raw = [tile("w4_raw%d" % b, [P, PACK, N], F32) for b in range(2)]
        syn_sb = [tile("syn%d" % b, [P, PACK, S], F32) for b in range(2)]

        nc.vector.memset(table_scales[:].bitcast(I32), 0)
        nc.gpsimd.memset(weight_scales[:].bitcast(I32), 0)
        make_identity(nc, identity[:])


        def load_scale_rows(dst, src, first):
            rows = src.bitcast(I32).rearrange("a (q r) c -> r q a c", r=4)
            for r in range(4):
                nc.sync.dma_start(
                    out=dst[first + r : P : QUAD, :].bitcast(I32).rearrange("q (a c) -> q a c", a=2), in_=rows[r]
                )

        def load_w1(a, b):
            nc.sync.dma_start(
                out=w1_raw[a, b][:],
                in_=w1[PASS * a : PASS * (a + 1), PASS * b : PASS * (b + 1)].rearrange("(p i) c -> p i c", i=PACK),
            )

        def load_table(a):
            nc.sync.dma_start(
                out=table_words[a][:].bitcast(I32), in_=tab_words[a].rearrange("p t i -> p (t i)").bitcast(I32)
            )

        def load_rows(dst, src, b, cols):
            rows = src[PASS * b : PASS * (b + 1), :].rearrange("(p t) c -> p t c", t=PACK)
            nc.sync.dma_start(out=dst[:, :, cols], in_=rows[:, :, cols])

        for l, src in enumerate((offs, offs2, offs3)):
            nc.sync.dma_start(lists[l][:], src)
        nc.sync.dma_start(
            out=w3_codes[:].bitcast(I32).rearrange("p (a c) -> p a c", a=2),
            in_=w3_words.bitcast(I32).rearrange("a p c -> p a c"),
        )
        load_scale_rows(weight_scales, w3_scales, 0)
        load_scale_rows(weight_scales, w2_scales, W2_ROW)
        load_scale_rows(table_scales, tab_scales, 0)
        load_table(0)
        nc.sync.dma_start(
            out=w2_codes[:].rearrange("p (a c) -> p a c", a=2),
            in_=w2_words.rearrange("a p c i -> p a (c i)").bitcast(I32),
        )
        load_table(1)
        for b in range(2):
            for a in range(2):
                load_w1(a, b)
        load_rows(w4_raw[0], w4, 0, slice(0, N))
        load_rows(syn_sb[0], syn, 0, slice(0, S))
        load_rows(w4_raw[1], w4, 1, slice(0, N))
        load_rows(syn_sb[1], syn, 1, slice(0, HALF))
        load_rows(syn_sb[1], syn, 1, slice(HALF, S))


        picked_words, picked_scales = {}, {}
        w1_q, w4_bf16, w4_q, h_bf16, h_q = {}, {}, {}, {}, {}
        larger, turned = {}, {}
        gather_order = (BY_W3, BY_W2, BY_W1)

        def gather_scales(a):
            for l in gather_order:
                picked_scales[l, a] = tile("picked_scales%d%d" % (l, a), [P, S], U8)
                nc.vector.tensor_copy(picked_scales[l, a][:], table_scales[:, a * T : (a + 1) * T].indirect(lists[l][:]))

        def gather_words(a):
            for l in gather_order:
                picked_words[l, a] = tile("picked_words%d%d" % (l, a), [P, S], U32)
                nc.vector.tensor_copy(picked_words[l, a][:], table_words[a][:].indirect(lists[l][:]))

        def quantise(name, src, width):
            codes = tile(name + "_codes", [P, width], U32)
            scales = tile(name + "_scales", [P, width], U8)
            nc.vector.quantize_mx(out=codes[:].bitcast(E4M3), scales=scales[:], in_=src[:])
            return codes, scales

        def round_w1(a, b, copy):
            rounded = tile("w1_bf16_%d%d" % (a, b), [P, PACK * PASS], BF16)
            copy(rounded[:].rearrange("p (c i) -> p c i", i=PACK), w1_raw[a, b][:].rearrange("p i c -> p c i"))
            return rounded

        def quantise_w1(a, b, rounded):
            w1_q[a, b] = quantise("w1_%d%d" % (a, b), rounded, PASS)

        def round_w4(b):
            w4_bf16[b] = tile("w4_bf16_%d" % b, [P, PACK * N], BF16)
            nc.scalar.copy(
                w4_bf16[b][:].rearrange("p (u m t) -> p u m t", u=PACK, t=PACK),
                w4_raw[b][:].rearrange("p t (m u) -> p u m t", u=PACK),
            )

        def quantise_w4(b):
            w4_q[b] = quantise("w4_%d" % b, w4_bf16[b], N)

        def first_stage_pass(bank, l, a, g, codes, scales, start, stop):
            cols = slice(g * P, (g + 1) * P)
            nc.tensor.matmul_mx(
                out=bank[:], lhsT=picked_words[l, a][:, cols].bitcast(E4M3), lhsT_scale=picked_scales[l, a][:, cols],
                rhs=codes, rhs_scale=scales, start=start, stop=stop,
            )

        def times_w3(banks, b, a):
            c = a * H + b * PASS
            codes = w3_codes[:, 2 * c : 2 * (c + PASS)].bitcast(E2M1)
            for g in range(GROUPS):
                first_stage_pass(banks[g], BY_W3, a, g, codes, weight_scales[:, c : c + PASS], a == 0, a == 1)

        def times_w2(bank, b, a, g):
            c = a * H + b * PASS
            codes = w2_codes[:, c : c + PASS].bitcast(E4M3)
            first_stage_pass(bank, BY_W2, a, g, codes, weight_scales[W2_ROW:P, c : c + PASS], a == 0, False)

        def times_w1(banks, b, a):
            codes, scales = w1_q[a, b]
            for g in range(GROUPS):
                first_stage_pass(banks[g], BY_W1, a, g, codes[:].bitcast(E4M3), scales[:], False, a == 1)

        def dealt(bank):
            return bank[:].rearrange("j (p t) -> j t p", t=PACK)

        def copy_pron(banks, b):
            for g in range(GROUPS):
                larger[b, g] = tile("larger%d%d" % (b, g), [P, PACK, P], F32)
                nc.scalar.copy(larger[b, g][:], dealt(banks[g]))

        def max_and_turn(banks, b, tag):
            for g in range(GROUPS):
                nc.vector.tensor_tensor(larger[b, g][:], dealt(banks[g]), larger[b, g][:], MAX)
            for g, bank in enumerate(four_banks(tag)):
                turned[b, g] = bank
                for t in range(PACK):
                    nc.tensor.transpose(bank[:, t * P : (t + 1) * P], larger[b, g][:, t, :], identity[:])

        def add_syn(b, half):
            h_bf16[b, half] = tile("h_bf16_%d%d" % (b, half), [P, PACK * HALF], BF16)
            for e in range(GROUPS // 2):
                g = GROUPS // 2 * half + e
                nc.vector.tensor_tensor(
                    h_bf16[b, half][:, e * PACK * P : (e + 1) * PACK * P].rearrange("p (j t) -> p j t", t=PACK),
                    turned[b, g][:].rearrange("p (t j) -> p j t", t=PACK),
                    syn_sb[b][:, :, g * P : (g + 1) * P].rearrange("p t j -> p j t"),
                    ADD,
                )

        def quantise_h(b, half):
            h_q[b, half] = quantise("h_%d%d" % (b, half), h_bf16[b, half], HALF)

        def times_w4(banks, b, half):
            w_codes, w_scales = w4_q[b]
            h_codes, h_scales = h_q[b, half]
            for u in range(PACK):
                nc.tensor.matmul_mx(
                    out=banks[2 * half + u // 2][:, (u % 2) * HALF : (u % 2 + 1) * HALF],
                    lhsT=w_codes[:, u * P : (u + 1) * P].bitcast(E4M3), lhsT_scale=w_scales[:, u * P : (u + 1) * P],
                    rhs=h_codes[:].bitcast(E4M3), rhs_scale=h_scales[:],
                    start=(b == 0 and u % 2 == 0), stop=(b == 1 and u % 2 == 1),
                )


        gather_scales(0)
        gather_words(0)
        gather_scales(1)
        pron0, ctx0 = four_banks("p"), four_banks("c")
        times_w3(pron0, 0, 0)
        for g in range(GROUPS):
            times_w2(ctx0[g], 0, 0, g)
        gather_words(1)
        times_w3(pron0, 0, 1)
        copy_pron(pron0, 0)
        for g in range(GROUPS):
            times_w2(ctx0[g], 0, 1, g)
        pron1 = four_banks("p")
        times_w3(pron1, 1, 0)
        times_w3(pron1, 1, 1)
        copy_pron(pron1, 1)
        quantise_w1(0, 0, round_w1(0, 0, nc.vector.tensor_copy))
        rounded = round_w1(1, 0, nc.vector.tensor_copy)
        times_w1(ctx0, 0, 0)
        quantise_w1(1, 0, rounded)
        times_w1(ctx0, 0, 1)
        ctx1 = four_banks("p")
        for g in range(GROUPS):
            for a in range(2):
                times_w2(ctx1[g], 1, a, g)
        rounded = round_w1(0, 1, nc.scalar.copy)
        max_and_turn(ctx0, 0, "c")
        quantise_w1(0, 1, rounded)
        times_w1(ctx1, 1, 0)
        quantise_w1(1, 1, round_w1(1, 1, nc.scalar.copy))
        times_w1(ctx1, 1, 1)
        round_w4(0)
        round_w4(1)
        max_and_turn(ctx1, 1, "p")


        for half in range(2):
            add_syn(0, half)
        for half in range(2):
            quantise_h(0, half)
        quantise_w4(0)
        y_banks = four_banks("c")
        for half in range(2):
            times_w4(y_banks, 0, half)

        y = [tile("y%d" % half, [P, PACK, HALF], F32) for half in range(2)]
        y_codes = tile("y_codes", [P, S], U32)
        y_scales = tile("y_scales", [P, S], U8)
        out_rows = out_0.rearrange("(p u) j -> p u j", u=PACK)
        out_words = out_1[0].rearrange("p m t -> p (m t)").bitcast(I32)
        out_scales = out_2[0].bitcast(I32)

        def hand_out(half, second_copy):
            cols = slice(half * HALF, (half + 1) * HALF)
            nc.scalar.copy(y[half][:, 0:2, :].rearrange("p u j -> p (u j)"), y_banks[2 * half][:])
            second_copy(y[half][:, 2:4, :].rearrange("p u j -> p (u j)"), y_banks[2 * half + 1][:])
            nc.sync.dma_start(out=out_rows[:, :, cols], in_=y[half][:])
            y_bf16 = tile("y_bf16_%d" % half, [P, PACK * HALF], BF16)
            nc.vector.tensor_copy(
                y_bf16[:].rearrange("p (j u) -> p j u", u=PACK), y[half][:].rearrange("p u j -> p j u")
            )
            nc.vector.quantize_mx(out=y_codes[:, cols].bitcast(E4M3), scales=y_scales[:, cols], in_=y_bf16[:])
            nc.sync.dma_start(out=out_words[:, cols], in_=y_codes[:, cols].bitcast(I32))

        add_syn(1, 0)
        quantise_w4(1)
        quantise_h(1, 0)
        times_w4(y_banks, 1, 0)
        add_syn(1, 1)
        quantise_h(1, 1)
        times_w4(y_banks, 1, 1)
        hand_out(0, nc.scalar.copy)
        hand_out(1, nc.vector.tensor_copy)
        for q in range(4):
            queue = nc.sync if q % 2 == 0 else nc.scalar
            queue.dma_start(
                out=out_scales[4 * q : 4 * q + 4, :], in_=y_scales[QUAD * q : QUAD * q + 4, :].bitcast(I32)
            )
